import numpy as np
import ml_dtypes


def mxq(x, axis, fmt="e4m3"):
    dtype, down = {"e4m3": (ml_dtypes.float8_e4m3fn, 7), "e5m2": (ml_dtypes.float8_e5m2, 14)}[fmt]
    v = np.moveaxis(np.asarray(x, np.float32).astype(ml_dtypes.bfloat16).astype(np.float64), axis, -1)
    blocks = v.reshape(v.shape[:-1] + (-1, 32))
    amax = np.abs(blocks).max(-1, keepdims=True)
    byte = np.maximum(np.where(amax > 0, np.frexp(amax)[1] - 1 + 127, 0) - down, 1)
    scale = np.exp2(byte - 127.0)
    codes = (blocks / scale).astype(np.float32).astype(dtype).astype(np.float64)
    return np.moveaxis((codes * scale).reshape(v.shape), -1, axis)


WIDE = False


def mx_kscale(k):
    if not WIDE:
        return np.ones(k)
    levels = np.array([10, -10, 5, -5, 0])
    if k % 512:
        return np.exp2(np.random.permutation(np.resize(levels, k // 32))).repeat(32)
    a = np.empty((k // 512, 16))
    for p in range(k // 512):
        a[p, :8] = np.random.permutation(np.resize(levels, 8))
        for g in range(8):
            far = levels[np.abs(levels - a[p, g]) >= 10]
            a[p, g + 8] = far[np.random.randint(len(far))]
    return np.exp2(a.ravel()).repeat(32)


def f64(x):
    return np.asarray(x).astype(np.float64)


def striped(idx):
    return np.tile(idx.reshape(-1, 16).T, (8, 1)).astype(np.uint16)


def unstriped(offs):
    return offs[:16].T.reshape(-1).astype(np.int64)


def striped8(idx):
    return np.concatenate([x.reshape(-1, 16).T for x in idx]).astype(np.uint16)


def runs(offs, k):
    lists = np.stack([offs[16 * r : 16 * r + 16].T.reshape(-1) for r in range(8)]).astype(np.int64)
    return lists[np.arange(k) % 512 // 64]


def pack_weight(w):
    k, n = w.shape
    w = f64(np.asarray(w, np.float32).astype(ml_dtypes.bfloat16)).reshape(k // 32, 32, n)
    amax = np.abs(w).max(1)
    byte = np.clip(np.where(amax > 0, np.frexp(amax)[1] - 1 + 127 - 7, 1), 1, 254)
    scaled = (w * np.exp2(127.0 - byte)[:, None, :]).reshape(k, n).astype(np.float32)
    words = np.ascontiguousarray(scaled.reshape(k // 512, 128, 4, n).transpose(0, 1, 3, 2)).astype(ml_dtypes.float8_e4m3fn).view(np.uint8)
    return words, np.ascontiguousarray(byte.astype(np.uint8).reshape(k // 512, 16, n))


def unpack_weight(words, scales):
    g, p, n, _ = words.shape
    vals = np.ascontiguousarray(words).view(ml_dtypes.float8_e4m3fn).astype(np.float64) * np.repeat(np.exp2(scales.astype(np.float64) - 127.0), 8, axis=1)[..., None]
    return vals.transpose(0, 1, 3, 2).reshape(g * 512, n)


E2M1 = np.array([0.0, 0.5, 1.0, 1.5, 2.0, 3.0, 4.0, 6.0, -0.0, -0.5, -1.0, -1.5, -2.0, -3.0, -4.0, -6.0])


def pack_fp4(w):
    k, n = w.shape
    w = f64(np.asarray(w, np.float32).astype(ml_dtypes.bfloat16)).reshape(k // 32, 32, n)
    amax = np.abs(w).max(1)
    mant, ex = np.frexp(amax / 6.0)
    byte = np.clip(np.where(amax > 0, np.where(mant > 0.5, ex, ex - 1) + 127, 1), 1, 254)
    scaled = (w * np.exp2(127.0 - byte)[:, None, :]).reshape(k, n).astype(np.float32)
    c = np.ascontiguousarray(scaled.reshape(k // 512, 128, 4, n).transpose(0, 1, 3, 2)).astype(ml_dtypes.float4_e2m1fn).view(np.uint8) & 0xF
    words = (c[..., 0::2] | (c[..., 1::2] << 4)).reshape(k // 512, 128, 2 * n)
    return np.ascontiguousarray(words), np.ascontiguousarray(byte.astype(np.uint8).reshape(k // 512, 16, n))


def unpack_fp4(words, scales):
    g, _, n = scales.shape
    words = np.ascontiguousarray(words).reshape(g, 128, n, 2)
    nib = np.empty((g, 128, n, 4), np.uint8)
    nib[..., 0::2] = words & 0xF
    nib[..., 1::2] = words >> 4
    vals = E2M1[nib] * np.repeat(np.exp2(scales.astype(np.float64) - 127.0), 8, axis=1)[..., None]
    return vals.transpose(0, 1, 3, 2).reshape(g * 512, n)


def sigmoid(v):
    return 1.0 / (1.0 + np.exp(-np.maximum(v, -700.0)))

def planes(y):
    n, m = y.shape
    v = y.astype(np.float32).astype(ml_dtypes.bfloat16).astype(np.float64).reshape(n // 32, 32, m)
    top = np.abs(v).max(1)
    byte = np.clip(np.where(top > 0, np.frexp(top)[1] - 1 + 127 - 7, 1), 1, 254)
    codes = (v * np.exp2(127.0 - byte)[:, None, :]).reshape(n, m).astype(np.float32).astype(ml_dtypes.float8_e4m3fn).view(np.uint8)
    words = codes.reshape(n // 512, 128, 4, m).transpose(0, 1, 3, 2)
    return np.ascontiguousarray(words), np.ascontiguousarray(byte.astype(np.uint8).reshape(n // 512, 16, m))


K, T, S, H, C = 512, 2048, 512, 512, 512


def setup_inputs():
    n = np.random.standard_normal
    s = mx_kscale(K)[:, None]
    packed_xT = pack_weight(n((K, T)) * s)
    packed_w1 = pack_fp4(n((K, H)) / np.sqrt(K) / s)
    packed_w2 = pack_fp4(n((K, H)) / np.sqrt(K) / s)
    return {
        "x_words": packed_xT[0],
        "x_scales": packed_xT[1],
        "w1_words": packed_w1[0],
        "w1_scales": packed_w1[1],
        "w2_words": packed_w2[0],
        "w2_scales": packed_w2[1],
        "gs": (np.random.uniform(0.5, 1.5, (K, 1)) / s).astype(np.float32),
        "offs": striped(np.random.permutation(T)[:S]),
        "two": striped(np.random.permutation(T)[:S]),
        "k0": striped8(np.stack([np.random.permutation(S) for _ in range(8)])),
        "k1": striped8(np.stack([np.random.permutation(S) for _ in range(8)])),
        "k2": striped8(np.stack([np.random.permutation(S) for _ in range(8)])),
        "k3": striped8(np.stack([np.random.permutation(S) for _ in range(8)])),
        "cand": striped(np.random.permutation(T)[:C]),
    }


def reference(x_words, x_scales, w1_words, w1_scales, w2_words, w2_scales, gs, offs, two, k0, k1, k2, k3, cand):
    x_cand = unpack_weight(x_words, x_scales)[:, unstriped(cand)]
    xq = unpack_weight(x_words, x_scales)[:, unstriped(offs)]
    y = unpack_fp4(w1_words, w1_scales).T @ xq
    b = y[np.arange(H)[:, None], runs(k1, H)]
    x_two = unpack_weight(x_words, x_scales)[:, unstriped(two)]
    t1 = sigmoid(unpack_fp4(w2_words, w2_scales).T @ x_two)
    c = y[np.arange(H)[:, None], runs(k2, H)]
    a = y[np.arange(H)[:, None], runs(k0, H)]
    c1 = 0.5 * (c - a)
    d = y[np.arange(H)[:, None], runs(k3, H)]
    c2 = a + 2.0 * c - (2.5 * b + 0.5 * d)
    c3 = 1.5 * (b - c) + 0.5 * (d - a)
    z = f64(gs) * (b + t1 * (c1 + t1 * (c2 + t1 * c3)))
    out_0 = 0.0625 * ((x_cand.T @ mxq(z, 0, "e4m3")))
    return (out_0,) + planes(out_0)

@@ -1,0 +1,184 @@
+from contextlib import ExitStack
+
+import concourse.mybir as mybir
+from concourse.masks import make_identity
+
+K, T, S, H, C = 512, 2048, 512, 512, 512
+FLOPS = 2 * K * H * S * 2 + 2 * K * C * S
+
+F32 = mybir.dt.float32
+BF16 = mybir.dt.bfloat16
+I32 = mybir.dt.int32
+U32 = mybir.dt.uint32
+U16 = mybir.dt.uint16
+U8 = mybir.dt.uint8
+FP8X4 = mybir.dt.float8_e4m3fn_x4
+FP4X4 = mybir.dt.float4_e2m1fn_x4
+ACT = mybir.ActivationFunctionType
+ALU = mybir.AluOpType
+
+P = 128
+R = 4
+QUART = 128
+NBLK = S // QUART
+D_ON_VECTOR = 2
+
+
+def tile_picked_catmull_none_po_kernel(
+    tc, x_words, x_scales, w1_words, w1_scales, w2_words, w2_scales, gs, offs, two, k0, k1, k2, k3, cand,
+    out_0, out_1, out_2,
+):
+    nc = tc.nc
+    with ExitStack() as ctx:
+        lists = ctx.enter_context(tc.tile_pool(name="lists", bufs=1))
+        keep = ctx.enter_context(tc.tile_pool(name="keep", bufs=1))
+        psum = ctx.enter_context(tc.psum_pool(name="psum", bufs=1))
+
+        def sb(shape, dtype, name):
+            return keep.tile(shape, dtype, name=name, align_bytes=64)
+
+        def load_list(src, name):
+            tl = lists.tile([P, S // 16], U16, name=name)
+            nc.sync.dma_start(tl[:], src)
+            return tl
+
+        def load_scale_rows(queue, dst, src):
+            for q in range(4):
+                queue.dma_start(dst[32 * q : 32 * q + 4, :].bitcast(I32), src[0, 4 * q : 4 * q + 4, :].bitcast(I32))
+
+        xs = sb([P, T], U8, "xs")
+        w1s_raw = sb([P, H], U8, "w1s_raw")
+        w1w_raw = sb([P, H], U16, "w1w_raw")
+        w2s = sb([P, H], U8, "w2s")
+        w2w = sb([P, H], U16, "w2w")
+        nc.vector.memset(xs[:].bitcast(I32), 0)
+        nc.gpsimd.memset(w1s_raw[:].bitcast(I32), 0)
+        ident = sb([P, P], F32, "ident")
+        make_identity(nc, ident[:])
+        nc.gpsimd.memset(w2s[:].bitcast(I32), 0)
+
+        xw = sb([P, T], U32, "xw")
+        nc.sync.dma_start(xw[:].bitcast(I32), x_words[0].rearrange("p n r -> p (n r)").bitcast(I32))
+        load_scale_rows(nc.sync, xs, x_scales)
+        l_offs = load_list(offs, "l_offs")
+        nc.sync.dma_start(w1w_raw[:].bitcast(I32), w1_words[0].bitcast(I32))
+        load_scale_rows(nc.sync, w1s_raw, w1_scales)
+        l_two = load_list(two, "l_two")
+        gain = sb([P, R], F32, "gain")
+        nc.sync.dma_start(gain[:], gs.rearrange("(p t) o -> p (t o)", t=R))
+        l_b = load_list(k1, "l_b")
+        l_c = load_list(k2, "l_c")
+        l_a = load_list(k0, "l_a")
+        l_d = load_list(k3, "l_d")
+        nc.sync.dma_start(w2w[:].bitcast(I32), w2_words[0].bitcast(I32))
+        load_scale_rows(nc.sync, w2s, w2_scales)
+        l_cand = load_list(cand, "l_cand")
+
+        def pick(lst, name):
+            words = sb([P, S], U32, name + "w")
+            scales = sb([P, S], U8, name + "s")
+            nc.vector.tensor_copy(scales[:], xs[:].indirect(lst[:]))
+            nc.vector.tensor_copy(words[:], xw[:].indirect(lst[:]))
+            return words, scales
+
+        xqw, xqs = pick(l_offs, "xq")
+        w1w = sb([P, H], U16, "w1w")
+        w1s = sb([P, H], U8, "w1s")
+        nc.scalar.copy(w1w[:].rearrange("p (t m) -> p t m", t=R), w1w_raw[:].rearrange("p (m t) -> p t m", t=R))
+        nc.vector.tensor_copy(w1s[:].rearrange("p (t m) -> p t m", t=R), w1s_raw[:].rearrange("p (m t) -> p t m", t=R))
+        xtw, xts = pick(l_two, "xt")
+
+        def bank(i, shape):
+            return psum.tile(shape, F32, name="bank%d" % i, tag="bank%d" % i)
+
+        y = []
+        for t in range(R):
+            acc = bank(t, [P, S])
+            nc.tensor.matmul_mx(acc[:], lhsT=w1w[:, t * P : (t + 1) * P].bitcast(U8).bitcast(FP4X4),
+                                lhsT_scale=w1s[:, t * P : (t + 1) * P],
+                                rhs=xqw[:].bitcast(FP8X4), rhs_scale=xqs[:], start=True, stop=True)
+            yt = sb([P, S], F32, "y%d" % t)
+            nc.scalar.activation(yt[:], acc[:], ACT.Copy, scale=gain[:, t : t + 1])
+            y.append(yt)
+
+        xcw = sb([P, C], U32, "xcw")
+        xcs = sb([P, C], U8, "xcs")
+
+        def pick_cand():
+            nc.vector.tensor_copy(xcs[:].rearrange("p (t m) -> p m t", t=R), xs[:].indirect(l_cand[:]))
+            nc.vector.tensor_copy(xcw[:].rearrange("p (t m) -> p m t", t=R), xw[:].indirect(l_cand[:]))
+
+        zb = sb([P, S, R], BF16, "zb")
+        zw = sb([P, S], U32, "zw")
+        zs = sb([P, S], U8, "zs")
+        ob = sb([P, S, R], BF16, "ob")
+        ow = sb([P, S], U32, "ow")
+        os_ = sb([P, S], U8, "osc")
+        out_rows = out_0.rearrange("(p t) j -> p t j", t=R)
+        out_words = out_1[0].rearrange("p n r -> p (n r)").bitcast(I32)
+        na = sb([P, R, QUART], F32, "na")
+        ncc = sb([P, R, QUART], F32, "ncc")
+        gd = sb([P, R, QUART], F32, "gd")
+
+        def turn_sum(dst, first, second):
+            nc.tensor.matmul(dst, lhsT=first, rhs=ident[:], start=True, stop=False, is_transpose=True)
+            nc.tensor.matmul(dst, lhsT=second, rhs=ident[:], start=False, stop=True, is_transpose=True)
+
+        for blk in range(NBLK):
+            cols = slice(blk * QUART, (blk + 1) * QUART)
+            lcols = slice(blk * QUART // 16, (blk + 1) * QUART // 16)
+            gb = sb([P, R, QUART], F32, "gb%d" % blk)
+            logit = bank(5 + blk % 3, [P, H])
+            nc.tensor.matmul_mx(logit[:], lhsT=xtw[:, cols].bitcast(FP8X4), lhsT_scale=xts[:, cols],
+                                rhs=w2w[:].bitcast(U8).bitcast(FP4X4), rhs_scale=w2s[:], start=True, stop=True)
+            bd, be, bg = bank(0, [P, R, P]), bank(1, [P, R, P]), bank(2, [P, R, P])
+            for t in range(R):
+                nc.vector.tensor_copy(gb[:, t, :], y[t][:].indirect(l_b[:, lcols]))
+                nc.scalar.activation(na[:, t, :], y[t][:].indirect(l_a[:, lcols]), ACT.Copy, scale=-1.0)
+                nc.scalar.activation(ncc[:, t, :], y[t][:].indirect(l_c[:, lcols]), ACT.Copy, scale=-1.0)
+                if t < D_ON_VECTOR:
+                    nc.vector.tensor_copy(gd[:, t, :], y[t][:].indirect(l_d[:, lcols]))
+                else:
+                    nc.scalar.activation(gd[:, t, :], y[t][:].indirect(l_d[:, lcols]), ACT.Copy)
+                turn_sum(be[:, t, :], na[:, t, :], gb[:, t, :])
+                turn_sum(bd[:, t, :], ncc[:, t, :], gb[:, t, :])
+                turn_sum(bg[:, t, :], na[:, t, :], gd[:, t, :])
+            tt = sb([P, R, P], F32, "tt%d" % blk)
+            qc = sb([P, R, P], F32, "qc%d" % blk)
+            qu = sb([P, R, P], F32, "qu%d" % blk)
+            nc.scalar.activation(tt[:], logit[:].rearrange("j (p t) -> j t p", t=R), ACT.Sigmoid)
+            nc.scalar.activation(qc[:], tt[:], ACT.Square, bias=-2.0, scale=3.0)
+            nc.scalar.activation(qu[:], tt[:], ACT.Square, bias=-1.0, scale=2.0)
+            if blk == 0:
+                pick_cand()
+            mm = sb([P, R, P], F32, "mm%d" % blk)
+            yy = sb([P, R, P], F32, "yy%d" % blk)
+            nc.vector.scalar_tensor_tensor(mm[:], bg[:], 0.125, tt[:], ALU.mult, ALU.mult)
+            nc.vector.scalar_tensor_tensor(yy[:], qc[:], -7.0, bd[:], ALU.add, ALU.mult)
+            nc.vector.scalar_tensor_tensor(mm[:], be[:], -0.125, mm[:], ALU.mult, ALU.add)
+            nc.vector.scalar_tensor_tensor(yy[:], yy[:], 1.0 / 6.0, tt[:], ALU.mult, ALU.mult)
+            nc.vector.scalar_tensor_tensor(mm[:], qu[:], -1.0, mm[:], ALU.add, ALU.mult)
+            bz = bank(3, [P, R, QUART])
+            for t in range(R):
+                turn_sum(bz[:, t, :], yy[:, t, :], mm[:, t, :])
+            nc.vector.tensor_tensor(
+                zb[:, cols, :].rearrange("p (c i) t -> p c t i", i=4),
+                bz[:].rearrange("p t (c i) -> p c t i", i=4),
+                gb[:].rearrange("p t (c i) -> p c t i", i=4), ALU.add)
+            nc.vector.quantize_mx(out=zw[:, cols].bitcast(FP8X4), scales=zs[:, cols],
+                                  in_=zb[:, cols, :].rearrange("p j t -> p (j t)"))
+            acc = bank(4, [P, R, QUART])
+            for t in range(R):
+                nc.tensor.matmul_mx(acc[:, t, :], lhsT=xcw[:, t * P : (t + 1) * P].bitcast(FP8X4),
+                                    lhsT_scale=xcs[:, t * P : (t + 1) * P],
+                                    rhs=zw[:, cols].bitcast(FP8X4), rhs_scale=zs[:, cols], start=True, stop=True)
+            of = sb([P, R, QUART], F32, "of%d" % blk)
+            nc.scalar.activation(ob[:, cols, :], acc[:].rearrange("p t j -> p j t"), ACT.Copy, scale=0.0625)
+            nc.scalar.activation(of[:], acc[:], ACT.Copy, scale=0.0625)
+            nc.sync.dma_start(out_rows[:, :, cols], of[:])
+            nc.vector.quantize_mx(out=ow[:, cols].bitcast(FP8X4), scales=os_[:, cols],
+                                  in_=ob[:, cols, :].rearrange("p j t -> p (j t)"))
+            nc.sync.dma_start(out_words[:, cols], ow[:, cols].bitcast(I32))
+        for q in range(4):
+            eng = nc.sync if q % 2 == 0 else nc.scalar
+            eng.dma_start(out_2[0, 4 * q : 4 * q + 4, :].bitcast(I32), os_[32 * q : 32 * q + 4, :].bitcast(I32))

@@ -21,7 +21,8 @@ P = 128
 R = 4
 QUART = 128
 NBLK = S // QUART
-D_ON_VECTOR = 2
+D_ON_VECTOR = (4, 3)
+OUT_BANKS = (7, 0, 1, 2)
 
 
 def tile_picked_catmull_none_po_kernel(
@@ -34,8 +35,8 @@ def tile_picked_catmull_none_po_kernel(
         keep = ctx.enter_context(tc.tile_pool(name="keep", bufs=1))
         psum = ctx.enter_context(tc.psum_pool(name="psum", bufs=1))
 
-        def sb(shape, dtype, name):
-            return keep.tile(shape, dtype, name=name, align_bytes=64)
+        def sb(shape, dtype, name, tag=None):
+            return keep.tile(shape, dtype, name=name, tag=tag or name, align_bytes=64)
 
         def load_list(src, name):
             tl = lists.tile([P, S // 16], U16, name=name)
@@ -57,25 +58,25 @@ def tile_picked_catmull_none_po_kernel(
         make_identity(nc, ident[:])
         nc.gpsimd.memset(w2s[:].bitcast(I32), 0)
 
+        nc.sync.dma_start(w1w_raw[:].bitcast(I32), w1_words[0].bitcast(I32))
+        l_offs = load_list(offs, "l_offs")
+        l_two = load_list(two, "l_two")
+        load_scale_rows(nc.sync, xs, x_scales)
         xw = sb([P, T], U32, "xw")
         nc.sync.dma_start(xw[:].bitcast(I32), x_words[0].rearrange("p n r -> p (n r)").bitcast(I32))
-        load_scale_rows(nc.sync, xs, x_scales)
-        l_offs = load_list(offs, "l_offs")
-        nc.sync.dma_start(w1w_raw[:].bitcast(I32), w1_words[0].bitcast(I32))
         load_scale_rows(nc.sync, w1s_raw, w1_scales)
-        l_two = load_list(two, "l_two")
         gain = sb([P, R], F32, "gain")
         nc.sync.dma_start(gain[:], gs.rearrange("(p t) o -> p (t o)", t=R))
         l_b = load_list(k1, "l_b")
-        l_c = load_list(k2, "l_c")
         l_a = load_list(k0, "l_a")
         l_d = load_list(k3, "l_d")
         nc.sync.dma_start(w2w[:].bitcast(I32), w2_words[0].bitcast(I32))
         load_scale_rows(nc.sync, w2s, w2_scales)
+        l_c = load_list(k2, "l_c")
         l_cand = load_list(cand, "l_cand")
 
-        def pick(lst, name):
-            words = sb([P, S], U32, name + "w")
+        def pick(lst, name, words_tag=None):
+            words = sb([P, S], U32, name + "w", tag=words_tag)
             scales = sb([P, S], U8, name + "s")
             nc.vector.tensor_copy(scales[:], xs[:].indirect(lst[:]))
             nc.vector.tensor_copy(words[:], xw[:].indirect(lst[:]))
@@ -86,7 +87,7 @@ def tile_picked_catmull_none_po_kernel(
         w1s = sb([P, H], U8, "w1s")
         nc.scalar.copy(w1w[:].rearrange("p (t m) -> p t m", t=R), w1w_raw[:].rearrange("p (m t) -> p t m", t=R))
         nc.vector.tensor_copy(w1s[:].rearrange("p (t m) -> p t m", t=R), w1s_raw[:].rearrange("p (m t) -> p t m", t=R))
-        xtw, xts = pick(l_two, "xt")
+        xtw, xts = pick(l_two, "xt", words_tag="w1s_raw")
 
         def bank(i, shape):
             return psum.tile(shape, F32, name="bank%d" % i, tag="bank%d" % i)
@@ -101,8 +102,8 @@ def tile_picked_catmull_none_po_kernel(
             nc.scalar.activation(yt[:], acc[:], ACT.Copy, scale=gain[:, t : t + 1])
             y.append(yt)
 
-        xcw = sb([P, C], U32, "xcw")
-        xcs = sb([P, C], U8, "xcs")
+        xcw = sb([P, C], U32, "xcw", tag="xqw")
+        xcs = sb([P, C], U8, "xcs", tag="xqs")
 
         def pick_cand():
             nc.vector.tensor_copy(xcs[:].rearrange("p (t m) -> p m t", t=R), xs[:].indirect(l_cand[:]))
@@ -116,58 +117,83 @@ def tile_picked_catmull_none_po_kernel(
         os_ = sb([P, S], U8, "osc")
         out_rows = out_0.rearrange("(p t) j -> p t j", t=R)
         out_words = out_1[0].rearrange("p n r -> p (n r)").bitcast(I32)
-        na = sb([P, R, QUART], F32, "na")
-        ncc = sb([P, R, QUART], F32, "ncc")
-        gd = sb([P, R, QUART], F32, "gd")
 
-        def turn_sum(dst, first, second):
-            nc.tensor.matmul(dst, lhsT=first, rhs=ident[:], start=True, stop=False, is_transpose=True)
-            nc.tensor.matmul(dst, lhsT=second, rhs=ident[:], start=False, stop=True, is_transpose=True)
+        def turn(dst, src, start, stop):
+            for t in range(R):
+                nc.tensor.matmul(dst[:, t, :], lhsT=src[:, t, :], rhs=ident[:], start=start and t == 0,
+                                 stop=stop and t == R - 1, is_transpose=True)
+
+        logits = []
+        for blk in range(NBLK):
+            cols = slice(blk * QUART, (blk + 1) * QUART)
+            logit = bank(4 + blk, [P, H])
+            nc.tensor.matmul_mx(logit[:], lhsT=xtw[:, cols].bitcast(FP8X4), lhsT_scale=xts[:, cols],
+                                rhs=w2w[:].bitcast(U8).bitcast(FP4X4), rhs_scale=w2s[:], start=True, stop=True)
+            logits.append(logit)
+        tts = [sb([P, R, P], F32, "tt%d" % blk) for blk in range(NBLK)]
+
+        def sigmoid(blk):
+            nc.scalar.activation(tts[blk][:], logits[blk][:].rearrange("j (p t) -> j t p", t=R), ACT.Sigmoid)
 
         for blk in range(NBLK):
             cols = slice(blk * QUART, (blk + 1) * QUART)
             lcols = slice(blk * QUART // 16, (blk + 1) * QUART // 16)
-            gb = sb([P, R, QUART], F32, "gb%d" % blk)
-            logit = bank(5 + blk % 3, [P, H])
-            nc.tensor.matmul_mx(logit[:], lhsT=xtw[:, cols].bitcast(FP8X4), lhsT_scale=xts[:, cols],
-                                rhs=w2w[:].bitcast(U8).bitcast(FP4X4), rhs_scale=w2s[:], start=True, stop=True)
-            bd, be, bg = bank(0, [P, R, P]), bank(1, [P, R, P]), bank(2, [P, R, P])
+            if blk % 2 == 0:
+                pcols = slice(blk * QUART // 16, (blk + 2) * QUART // 16)
+                gb2 = sb([P, R, 2 * QUART], F32, "gb%d" % blk)
+                gd2 = sb([P, R, 2 * QUART], F32, "gd%d" % blk)
+                for t in range(R):
+                    nc.vector.tensor_copy(gb2[:, t, :], y[t][:].indirect(l_b[:, pcols]))
+                for t in range(R):
+                    if t < D_ON_VECTOR[blk // 2]:
+                        nc.vector.tensor_copy(gd2[:, t, :], y[t][:].indirect(l_d[:, pcols]))
+            own = slice(blk % 2 * QUART, (blk % 2 + 1) * QUART)
+            gb, gd = gb2[:, :, own], gd2[:, :, own]
+            na, ncc = [sb([P, R, QUART], F32, n + str(blk)) for n in ("na", "ncc")]
+            first = 4 * (blk % 2)
+            be, bg, bd = bank(first, [P, R, P]), bank(first + 1, [P, R, P]), bank(first + 2, [P, R, P])
             for t in range(R):
-                nc.vector.tensor_copy(gb[:, t, :], y[t][:].indirect(l_b[:, lcols]))
                 nc.scalar.activation(na[:, t, :], y[t][:].indirect(l_a[:, lcols]), ACT.Copy, scale=-1.0)
-                nc.scalar.activation(ncc[:, t, :], y[t][:].indirect(l_c[:, lcols]), ACT.Copy, scale=-1.0)
-                if t < D_ON_VECTOR:
-                    nc.vector.tensor_copy(gd[:, t, :], y[t][:].indirect(l_d[:, lcols]))
-                else:
-                    nc.scalar.activation(gd[:, t, :], y[t][:].indirect(l_d[:, lcols]), ACT.Copy)
-                turn_sum(be[:, t, :], na[:, t, :], gb[:, t, :])
-                turn_sum(bd[:, t, :], ncc[:, t, :], gb[:, t, :])
-                turn_sum(bg[:, t, :], na[:, t, :], gd[:, t, :])
-            tt = sb([P, R, P], F32, "tt%d" % blk)
+            for t in range(D_ON_VECTOR[blk // 2], R):
+                nc.scalar.activation(gd[:, t, :], y[t][:].indirect(l_d[:, lcols]), ACT.Copy)
+            tt = tts[blk]
+            if blk == 0:
+                sigmoid(0)
             qc = sb([P, R, P], F32, "qc%d" % blk)
             qu = sb([P, R, P], F32, "qu%d" % blk)
-            nc.scalar.activation(tt[:], logit[:].rearrange("j (p t) -> j t p", t=R), ACT.Sigmoid)
-            nc.scalar.activation(qc[:], tt[:], ACT.Square, bias=-2.0, scale=3.0)
             nc.scalar.activation(qu[:], tt[:], ACT.Square, bias=-1.0, scale=2.0)
+            nc.scalar.activation(qc[:], tt[:], ACT.Square, bias=-2.0, scale=3.0)
+            for t in range(R):
+                nc.scalar.activation(ncc[:, t, :], y[t][:].indirect(l_c[:, lcols]), ACT.Copy, scale=-1.0)
+            turn(be, gb, True, False)
+            turn(be, na, False, True)
+            turn(bg, na, True, False)
+            turn(bg, gd, False, True)
+            turn(bd, gb, True, False)
+            turn(bd, ncc, False, True)
             if blk == 0:
+                for later in range(1, NBLK):
+                    sigmoid(later)
                 pick_cand()
             mm = sb([P, R, P], F32, "mm%d" % blk)
             yy = sb([P, R, P], F32, "yy%d" % blk)
             nc.vector.scalar_tensor_tensor(mm[:], bg[:], 0.125, tt[:], ALU.mult, ALU.mult)
-            nc.vector.scalar_tensor_tensor(yy[:], qc[:], -7.0, bd[:], ALU.add, ALU.mult)
             nc.vector.scalar_tensor_tensor(mm[:], be[:], -0.125, mm[:], ALU.mult, ALU.add)
-            nc.vector.scalar_tensor_tensor(yy[:], yy[:], 1.0 / 6.0, tt[:], ALU.mult, ALU.mult)
             nc.vector.scalar_tensor_tensor(mm[:], qu[:], -1.0, mm[:], ALU.add, ALU.mult)
+            nc.vector.scalar_tensor_tensor(yy[:], qc[:], -7.0, bd[:], ALU.add, ALU.mult)
+            nc.vector.scalar_tensor_tensor(yy[:], yy[:], 1.0 / 6.0, tt[:], ALU.mult, ALU.mult)
             bz = bank(3, [P, R, QUART])
-            for t in range(R):
-                turn_sum(bz[:, t, :], yy[:, t, :], mm[:, t, :])
+            turn(bz, mm, True, False)
+            turn(bz, yy, False, True)
             nc.vector.tensor_tensor(
                 zb[:, cols, :].rearrange("p (c i) t -> p c t i", i=4),
                 bz[:].rearrange("p t (c i) -> p c t i", i=4),
-                gb[:].rearrange("p t (c i) -> p c t i", i=4), ALU.add)
+                gb.rearrange("p t (c i) -> p c t i", i=4), ALU.add)
             nc.vector.quantize_mx(out=zw[:, cols].bitcast(FP8X4), scales=zs[:, cols],
                                   in_=zb[:, cols, :].rearrange("p j t -> p (j t)"))
-            acc = bank(4, [P, R, QUART])
+        for blk in range(NBLK):
+            cols = slice(blk * QUART, (blk + 1) * QUART)
+            acc = bank(OUT_BANKS[blk], [P, R, QUART])
             for t in range(R):
                 nc.tensor.matmul_mx(acc[:, t, :], lhsT=xcw[:, t * P : (t + 1) * P].bitcast(FP8X4),
                                     lhsT_scale=xcs[:, t * P : (t + 1) * P],

@@ -22,7 +22,8 @@ R = 4
 QUART = 128
 NBLK = S // QUART
 D_ON_VECTOR = (4, 3)
-OUT_BANKS = (7, 0, 1, 2)
+BACK_BANKS = (3, 3, 3, 2)
+OUT_BANKS = (7, 0, 1, 4)
 
 
 def tile_picked_catmull_none_po_kernel(
@@ -43,51 +44,52 @@ def tile_picked_catmull_none_po_kernel(
             nc.sync.dma_start(tl[:], src)
             return tl
 
-        def load_scale_rows(queue, dst, src):
+        def load_scale_rows(queues, dst, src):
             for q in range(4):
-                queue.dma_start(dst[32 * q : 32 * q + 4, :].bitcast(I32), src[0, 4 * q : 4 * q + 4, :].bitcast(I32))
+                queues[q].dma_start(dst[32 * q : 32 * q + 4, :].bitcast(I32), src[0, 4 * q : 4 * q + 4, :].bitcast(I32))
 
         xs = sb([P, T], U8, "xs")
-        w1s_raw = sb([P, H], U8, "w1s_raw")
-        w1w_raw = sb([P, H], U16, "w1w_raw")
-        w2s = sb([P, H], U8, "w2s")
-        w2w = sb([P, H], U16, "w2w")
         nc.vector.memset(xs[:].bitcast(I32), 0)
-        nc.gpsimd.memset(w1s_raw[:].bitcast(I32), 0)
         ident = sb([P, P], F32, "ident")
         make_identity(nc, ident[:])
-        nc.gpsimd.memset(w2s[:].bitcast(I32), 0)
 
-        nc.sync.dma_start(w1w_raw[:].bitcast(I32), w1_words[0].bitcast(I32))
+        w1s_raw = sb([P, H], U8, "w1s_raw")
+        w2s = sb([P, H], U8, "w2s")
+        nc.gpsimd.memset(w1s_raw[:], 0)
+        nc.gpsimd.memset(w2s[:], 0)
+
         l_offs = load_list(offs, "l_offs")
+        w1w_raw = sb([P, H], U16, "w1w_raw")
+        load_scale_rows((nc.sync, nc.sync, nc.scalar, nc.scalar), xs[:], x_scales)
         l_two = load_list(two, "l_two")
-        load_scale_rows(nc.sync, xs, x_scales)
         xw = sb([P, T], U32, "xw")
         nc.sync.dma_start(xw[:].bitcast(I32), x_words[0].rearrange("p n r -> p (n r)").bitcast(I32))
-        load_scale_rows(nc.sync, w1s_raw, w1_scales)
+        load_scale_rows([nc.scalar] * 4, w1s_raw[:], w1_scales)
+        nc.sync.dma_start(w1w_raw[:].bitcast(I32), w1_words[0].bitcast(I32))
+        w1w = sb([P, H], U16, "w1w")
+        nc.scalar.copy(w1w[:].rearrange("p (t m) -> p t m", t=R), w1w_raw[:].rearrange("p (m t) -> p t m", t=R))
+        load_scale_rows([nc.scalar] * 4, w2s[:], w2_scales)
         gain = sb([P, R], F32, "gain")
         nc.sync.dma_start(gain[:], gs.rearrange("(p t) o -> p (t o)", t=R))
+        l_cand = load_list(cand, "l_cand")
         l_b = load_list(k1, "l_b")
         l_a = load_list(k0, "l_a")
         l_d = load_list(k3, "l_d")
+        w2w = sb([P, H], U16, "w2w")
         nc.sync.dma_start(w2w[:].bitcast(I32), w2_words[0].bitcast(I32))
-        load_scale_rows(nc.sync, w2s, w2_scales)
         l_c = load_list(k2, "l_c")
-        l_cand = load_list(cand, "l_cand")
 
-        def pick(lst, name, words_tag=None):
-            words = sb([P, S], U32, name + "w", tag=words_tag)
+        def pick(lst, name):
+            words = sb([P, S], U32, name + "w")
             scales = sb([P, S], U8, name + "s")
             nc.vector.tensor_copy(scales[:], xs[:].indirect(lst[:]))
             nc.vector.tensor_copy(words[:], xw[:].indirect(lst[:]))
             return words, scales
 
         xqw, xqs = pick(l_offs, "xq")
-        w1w = sb([P, H], U16, "w1w")
         w1s = sb([P, H], U8, "w1s")
-        nc.scalar.copy(w1w[:].rearrange("p (t m) -> p t m", t=R), w1w_raw[:].rearrange("p (m t) -> p t m", t=R))
-        nc.vector.tensor_copy(w1s[:].rearrange("p (t m) -> p t m", t=R), w1s_raw[:].rearrange("p (m t) -> p t m", t=R))
-        xtw, xts = pick(l_two, "xt", words_tag="w1s_raw")
+        nc.gpsimd.tensor_copy(w1s[:].rearrange("p (t m) -> p t m", t=R), w1s_raw[:].rearrange("p (m t) -> p t m", t=R))
+        xtw, xts = pick(l_two, "xt")
 
         def bank(i, shape):
             return psum.tile(shape, F32, name="bank%d" % i, tag="bank%d" % i)
@@ -102,8 +104,8 @@ def tile_picked_catmull_none_po_kernel(
             nc.scalar.activation(yt[:], acc[:], ACT.Copy, scale=gain[:, t : t + 1])
             y.append(yt)
 
-        xcw = sb([P, C], U32, "xcw", tag="xqw")
-        xcs = sb([P, C], U8, "xcs", tag="xqs")
+        xcw = sb([P, C], U32, "xcw")
+        xcs = sb([P, C], U8, "xcs")
 
         def pick_cand():
             nc.vector.tensor_copy(xcs[:].rearrange("p (t m) -> p m t", t=R), xs[:].indirect(l_cand[:]))
@@ -123,6 +125,17 @@ def tile_picked_catmull_none_po_kernel(
                 nc.tensor.matmul(dst[:, t, :], lhsT=src[:, t, :], rhs=ident[:], start=start and t == 0,
                                  stop=stop and t == R - 1, is_transpose=True)
 
+        scores = {}
+
+        def score(blk):
+            cols = slice(blk * QUART, (blk + 1) * QUART)
+            acc = bank(OUT_BANKS[blk], [P, R, QUART])
+            for t in range(R):
+                nc.tensor.matmul_mx(acc[:, t, :], lhsT=xcw[:, t * P : (t + 1) * P].bitcast(FP8X4),
+                                    lhsT_scale=xcs[:, t * P : (t + 1) * P],
+                                    rhs=zw[:, cols].bitcast(FP8X4), rhs_scale=zs[:, cols], start=True, stop=True)
+            scores[blk] = acc
+
         logits = []
         for blk in range(NBLK):
             cols = slice(blk * QUART, (blk + 1) * QUART)
@@ -135,23 +148,26 @@ def tile_picked_catmull_none_po_kernel(
         def sigmoid(blk):
             nc.scalar.activation(tts[blk][:], logits[blk][:].rearrange("j (p t) -> j t p", t=R), ACT.Sigmoid)
 
-        for blk in range(NBLK):
-            cols = slice(blk * QUART, (blk + 1) * QUART)
+        knots_b, knots_d, sums, terms, quads = {}, {}, {}, {}, {}
+
+        def fetch_pair(blk):
+            pcols = slice(blk * QUART // 16, (blk + 2) * QUART // 16)
+            gb2 = sb([P, R, 2 * QUART], F32, "gb%d" % blk, tag="xtw" if blk else None)
+            gd2 = sb([P, R, 2 * QUART], F32, "gd%d" % blk, tag="xts" if blk else None)
+            for t in range(R):
+                nc.vector.tensor_copy(gb2[:, t, :], y[t][:].indirect(l_b[:, pcols]))
+            for t in range(D_ON_VECTOR[blk // 2]):
+                nc.vector.tensor_copy(gd2[:, t, :], y[t][:].indirect(l_d[:, pcols]))
+            for e in range(2):
+                own = slice(e * QUART, (e + 1) * QUART)
+                knots_b[blk + e], knots_d[blk + e] = gb2[:, :, own], gd2[:, :, own]
+
+        def forward(blk):
             lcols = slice(blk * QUART // 16, (blk + 1) * QUART // 16)
-            if blk % 2 == 0:
-                pcols = slice(blk * QUART // 16, (blk + 2) * QUART // 16)
-                gb2 = sb([P, R, 2 * QUART], F32, "gb%d" % blk)
-                gd2 = sb([P, R, 2 * QUART], F32, "gd%d" % blk)
-                for t in range(R):
-                    nc.vector.tensor_copy(gb2[:, t, :], y[t][:].indirect(l_b[:, pcols]))
-                for t in range(R):
-                    if t < D_ON_VECTOR[blk // 2]:
-                        nc.vector.tensor_copy(gd2[:, t, :], y[t][:].indirect(l_d[:, pcols]))
-            own = slice(blk % 2 * QUART, (blk % 2 + 1) * QUART)
-            gb, gd = gb2[:, :, own], gd2[:, :, own]
+            gb, gd = knots_b[blk], knots_d[blk]
             na, ncc = [sb([P, R, QUART], F32, n + str(blk)) for n in ("na", "ncc")]
             first = 4 * (blk % 2)
-            be, bg, bd = bank(first, [P, R, P]), bank(first + 1, [P, R, P]), bank(first + 2, [P, R, P])
+            bg, bd, be = bank(first, [P, R, P]), bank(first + 1, [P, R, P]), bank(first + 2, [P, R, P])
             for t in range(R):
                 nc.scalar.activation(na[:, t, :], y[t][:].indirect(l_a[:, lcols]), ACT.Copy, scale=-1.0)
             for t in range(D_ON_VECTOR[blk // 2], R):
@@ -161,50 +177,87 @@ def tile_picked_catmull_none_po_kernel(
                 sigmoid(0)
             qc = sb([P, R, P], F32, "qc%d" % blk)
             qu = sb([P, R, P], F32, "qu%d" % blk)
-            nc.scalar.activation(qu[:], tt[:], ACT.Square, bias=-1.0, scale=2.0)
-            nc.scalar.activation(qc[:], tt[:], ACT.Square, bias=-2.0, scale=3.0)
             for t in range(R):
                 nc.scalar.activation(ncc[:, t, :], y[t][:].indirect(l_c[:, lcols]), ACT.Copy, scale=-1.0)
-            turn(be, gb, True, False)
-            turn(be, na, False, True)
-            turn(bg, na, True, False)
-            turn(bg, gd, False, True)
+            nc.scalar.activation(qc[:], tt[:], ACT.Square, bias=-2.0, scale=3.0)
+            nc.scalar.activation(qu[:], tt[:], ACT.Square, bias=-1.0, scale=2.0)
+            turn(bg, gd, True, False)
             turn(bd, gb, True, False)
+            turn(be, gb, True, False)
+            turn(bg, na, False, True)
             turn(bd, ncc, False, True)
-            if blk == 0:
-                for later in range(1, NBLK):
-                    sigmoid(later)
-                pick_cand()
+            turn(be, na, False, True)
+            sums[blk] = be, bg, bd
+            quads[blk] = qu, qc
+
+        def curve(blk):
+            be, bg, bd = sums[blk]
+            qu, qc = quads[blk]
+            tt = tts[blk]
             mm = sb([P, R, P], F32, "mm%d" % blk)
             yy = sb([P, R, P], F32, "yy%d" % blk)
             nc.vector.scalar_tensor_tensor(mm[:], bg[:], 0.125, tt[:], ALU.mult, ALU.mult)
-            nc.vector.scalar_tensor_tensor(mm[:], be[:], -0.125, mm[:], ALU.mult, ALU.add)
-            nc.vector.scalar_tensor_tensor(mm[:], qu[:], -1.0, mm[:], ALU.add, ALU.mult)
             nc.vector.scalar_tensor_tensor(yy[:], qc[:], -7.0, bd[:], ALU.add, ALU.mult)
+            nc.vector.scalar_tensor_tensor(mm[:], be[:], -0.125, mm[:], ALU.mult, ALU.add)
             nc.vector.scalar_tensor_tensor(yy[:], yy[:], 1.0 / 6.0, tt[:], ALU.mult, ALU.mult)
-            bz = bank(3, [P, R, QUART])
-            turn(bz, mm, True, False)
-            turn(bz, yy, False, True)
+            nc.vector.scalar_tensor_tensor(mm[:], qu[:], -1.0, mm[:], ALU.add, ALU.mult)
+            terms[blk] = mm, yy
+
+        def backward(blk):
+            cols = slice(blk * QUART, (blk + 1) * QUART)
+            mm, yy = terms[blk]
+            bz = bank(BACK_BANKS[blk], [P, R, QUART])
+            turn(bz, yy, True, False)
+            turn(bz, mm, False, True)
             nc.vector.tensor_tensor(
                 zb[:, cols, :].rearrange("p (c i) t -> p c t i", i=4),
                 bz[:].rearrange("p t (c i) -> p c t i", i=4),
-                gb.rearrange("p t (c i) -> p c t i", i=4), ALU.add)
+                knots_b[blk].rearrange("p t (c i) -> p c t i", i=4), ALU.add)
             nc.vector.quantize_mx(out=zw[:, cols].bitcast(FP8X4), scales=zs[:, cols],
                                   in_=zb[:, cols, :].rearrange("p j t -> p (j t)"))
-        for blk in range(NBLK):
+
+        def finish(blk):
             cols = slice(blk * QUART, (blk + 1) * QUART)
-            acc = bank(OUT_BANKS[blk], [P, R, QUART])
-            for t in range(R):
-                nc.tensor.matmul_mx(acc[:, t, :], lhsT=xcw[:, t * P : (t + 1) * P].bitcast(FP8X4),
-                                    lhsT_scale=xcs[:, t * P : (t + 1) * P],
-                                    rhs=zw[:, cols].bitcast(FP8X4), rhs_scale=zs[:, cols], start=True, stop=True)
+            acc = scores[blk]
             of = sb([P, R, QUART], F32, "of%d" % blk)
             nc.scalar.activation(ob[:, cols, :], acc[:].rearrange("p t j -> p j t"), ACT.Copy, scale=0.0625)
             nc.scalar.activation(of[:], acc[:], ACT.Copy, scale=0.0625)
             nc.sync.dma_start(out_rows[:, :, cols], of[:])
+
+        def hand_on(first, last):
+            cols = slice(first * QUART, (last + 1) * QUART)
             nc.vector.quantize_mx(out=ow[:, cols].bitcast(FP8X4), scales=os_[:, cols],
                                   in_=ob[:, cols, :].rearrange("p j t -> p (j t)"))
             nc.sync.dma_start(out_words[:, cols], ow[:, cols].bitcast(I32))
+
+        pick_cand()
+        fetch_pair(0)
+        forward(0)
+        sigmoid(1)
+        sigmoid(2)
+        sigmoid(3)
+        fetch_pair(2)
+        forward(1)
+        curve(0)
+        backward(0)
+        forward(2)
+        curve(1)
+        score(0)
+        backward(1)
+        forward(3)
+        curve(2)
+        score(1)
+        backward(2)
+        curve(3)
+        backward(3)
+        score(2)
+        score(3)
+        finish(0)
+        finish(1)
+        finish(2)
+        hand_on(0, 2)
+        finish(3)
+        hand_on(3, 3)
         for q in range(4):
             eng = nc.sync if q % 2 == 0 else nc.scalar
             eng.dma_start(out_2[0, 4 * q : 4 * q + 4, :].bitcast(I32), os_[32 * q : 32 * q + 4, :].bitcast(I32))

from contextlib import ExitStack

import concourse.mybir as mybir
from concourse.masks import make_identity

K, T, S, H, C = 512, 2048, 512, 512, 512
FLOPS = 2 * K * H * S * 2 + 2 * K * C * S

F32 = mybir.dt.float32
BF16 = mybir.dt.bfloat16
I32 = mybir.dt.int32
U32 = mybir.dt.uint32
U16 = mybir.dt.uint16
U8 = mybir.dt.uint8
FP8X4 = mybir.dt.float8_e4m3fn_x4
FP4X4 = mybir.dt.float4_e2m1fn_x4
ACT = mybir.ActivationFunctionType
ALU = mybir.AluOpType

P = 128
R = 4
QUART = 128
NBLK = S // QUART
D_ON_VECTOR = (4, 3)
BACK_BANKS = (3, 3, 3, 2)
OUT_BANKS = (7, 0, 1, 4)


def tile_picked_catmull_none_po_kernel(
    tc, x_words, x_scales, w1_words, w1_scales, w2_words, w2_scales, gs, offs, two, k0, k1, k2, k3, cand,
    out_0, out_1, out_2,
):
    nc = tc.nc
    with ExitStack() as ctx:
        lists = ctx.enter_context(tc.tile_pool(name="lists", bufs=1))
        keep = ctx.enter_context(tc.tile_pool(name="keep", bufs=1))
        psum = ctx.enter_context(tc.psum_pool(name="psum", bufs=1))

        def sb(shape, dtype, name, tag=None):
            return keep.tile(shape, dtype, name=name, tag=tag or name, align_bytes=64)

        def load_list(src, name):
            tl = lists.tile([P, S // 16], U16, name=name)
            nc.sync.dma_start(tl[:], src)
            return tl

        def load_scale_rows(queues, dst, src):
            for q in range(4):
                queues[q].dma_start(dst[32 * q : 32 * q + 4, :].bitcast(I32), src[0, 4 * q : 4 * q + 4, :].bitcast(I32))

        xs = sb([P, T], U8, "xs")
        nc.vector.memset(xs[:].bitcast(I32), 0)
        ident = sb([P, P], F32, "ident")
        make_identity(nc, ident[:])

        w1s_raw = sb([P, H], U8, "w1s_raw")
        w2s = sb([P, H], U8, "w2s")
        nc.gpsimd.memset(w1s_raw[:], 0)
        nc.gpsimd.memset(w2s[:], 0)

        l_offs = load_list(offs, "l_offs")
        w1w_raw = sb([P, H], U16, "w1w_raw")
        load_scale_rows((nc.sync, nc.sync, nc.scalar, nc.scalar), xs[:], x_scales)
        l_two = load_list(two, "l_two")
        xw = sb([P, T], U32, "xw")
        nc.sync.dma_start(xw[:].bitcast(I32), x_words[0].rearrange("p n r -> p (n r)").bitcast(I32))
        load_scale_rows([nc.scalar] * 4, w1s_raw[:], w1_scales)
        nc.sync.dma_start(w1w_raw[:].bitcast(I32), w1_words[0].bitcast(I32))
        w1w = sb([P, H], U16, "w1w")
        nc.scalar.copy(w1w[:].rearrange("p (t m) -> p t m", t=R), w1w_raw[:].rearrange("p (m t) -> p t m", t=R))
        load_scale_rows([nc.scalar] * 4, w2s[:], w2_scales)
        gain = sb([P, R], F32, "gain")
        nc.sync.dma_start(gain[:], gs.rearrange("(p t) o -> p (t o)", t=R))
        l_cand = load_list(cand, "l_cand")
        l_b = load_list(k1, "l_b")
        l_a = load_list(k0, "l_a")
        l_d = load_list(k3, "l_d")
        w2w = sb([P, H], U16, "w2w")
        nc.sync.dma_start(w2w[:].bitcast(I32), w2_words[0].bitcast(I32))
        l_c = load_list(k2, "l_c")

        def pick(lst, name):
            words = sb([P, S], U32, name + "w")
            scales = sb([P, S], U8, name + "s")
            nc.vector.tensor_copy(scales[:], xs[:].indirect(lst[:]))
            nc.vector.tensor_copy(words[:], xw[:].indirect(lst[:]))
            return words, scales

        xqw, xqs = pick(l_offs, "xq")
        w1s = sb([P, H], U8, "w1s")
        nc.gpsimd.tensor_copy(w1s[:].rearrange("p (t m) -> p t m", t=R), w1s_raw[:].rearrange("p (m t) -> p t m", t=R))
        xtw, xts = pick(l_two, "xt")

        def bank(i, shape):
            return psum.tile(shape, F32, name="bank%d" % i, tag="bank%d" % i)

        y = []
        for t in range(R):
            acc = bank(t, [P, S])
            nc.tensor.matmul_mx(acc[:], lhsT=w1w[:, t * P : (t + 1) * P].bitcast(U8).bitcast(FP4X4),
                                lhsT_scale=w1s[:, t * P : (t + 1) * P],
                                rhs=xqw[:].bitcast(FP8X4), rhs_scale=xqs[:], start=True, stop=True)
            yt = sb([P, S], F32, "y%d" % t)
            nc.scalar.activation(yt[:], acc[:], ACT.Copy, scale=gain[:, t : t + 1])
            y.append(yt)

        xcw = sb([P, C], U32, "xcw")
        xcs = sb([P, C], U8, "xcs")

        def pick_cand():
            nc.vector.tensor_copy(xcs[:].rearrange("p (t m) -> p m t", t=R), xs[:].indirect(l_cand[:]))
            nc.vector.tensor_copy(xcw[:].rearrange("p (t m) -> p m t", t=R), xw[:].indirect(l_cand[:]))

        zb = sb([P, S, R], BF16, "zb")
        zw = sb([P, S], U32, "zw")
        zs = sb([P, S], U8, "zs")
        ob = sb([P, S, R], BF16, "ob")
        ow = sb([P, S], U32, "ow")
        os_ = sb([P, S], U8, "osc")
        out_rows = out_0.rearrange("(p t) j -> p t j", t=R)
        out_words = out_1[0].rearrange("p n r -> p (n r)").bitcast(I32)

        def turn(dst, src, start, stop):
            for t in range(R):
                nc.tensor.matmul(dst[:, t, :], lhsT=src[:, t, :], rhs=ident[:], start=start and t == 0,
                                 stop=stop and t == R - 1, is_transpose=True)

        scores = {}

        def score(blk):
            cols = slice(blk * QUART, (blk + 1) * QUART)
            acc = bank(OUT_BANKS[blk], [P, R, QUART])
            for t in range(R):
                nc.tensor.matmul_mx(acc[:, t, :], lhsT=xcw[:, t * P : (t + 1) * P].bitcast(FP8X4),
                                    lhsT_scale=xcs[:, t * P : (t + 1) * P],
                                    rhs=zw[:, cols].bitcast(FP8X4), rhs_scale=zs[:, cols], start=True, stop=True)
            scores[blk] = acc

        logits = []
        for blk in range(NBLK):
            cols = slice(blk * QUART, (blk + 1) * QUART)
            logit = bank(4 + blk, [P, H])
            nc.tensor.matmul_mx(logit[:], lhsT=xtw[:, cols].bitcast(FP8X4), lhsT_scale=xts[:, cols],
                                rhs=w2w[:].bitcast(U8).bitcast(FP4X4), rhs_scale=w2s[:], start=True, stop=True)
            logits.append(logit)
        tts = [sb([P, R, P], F32, "tt%d" % blk) for blk in range(NBLK)]

        def sigmoid(blk):
            nc.scalar.activation(tts[blk][:], logits[blk][:].rearrange("j (p t) -> j t p", t=R), ACT.Sigmoid)

        knots_b, knots_d, sums, terms, quads = {}, {}, {}, {}, {}

        def fetch_pair(blk):
            pcols = slice(blk * QUART // 16, (blk + 2) * QUART // 16)
            gb2 = sb([P, R, 2 * QUART], F32, "gb%d" % blk, tag="xtw" if blk else None)
            gd2 = sb([P, R, 2 * QUART], F32, "gd%d" % blk, tag="xts" if blk else None)
            for t in range(R):
                nc.vector.tensor_copy(gb2[:, t, :], y[t][:].indirect(l_b[:, pcols]))
            for t in range(D_ON_VECTOR[blk // 2]):
                nc.vector.tensor_copy(gd2[:, t, :], y[t][:].indirect(l_d[:, pcols]))
            for e in range(2):
                own = slice(e * QUART, (e + 1) * QUART)
                knots_b[blk + e], knots_d[blk + e] = gb2[:, :, own], gd2[:, :, own]

        def forward(blk):
            lcols = slice(blk * QUART // 16, (blk + 1) * QUART // 16)
            gb, gd = knots_b[blk], knots_d[blk]
            na, ncc = [sb([P, R, QUART], F32, n + str(blk)) for n in ("na", "ncc")]
            first = 4 * (blk % 2)
            bg, bd, be = bank(first, [P, R, P]), bank(first + 1, [P, R, P]), bank(first + 2, [P, R, P])
            for t in range(R):
                nc.scalar.activation(na[:, t, :], y[t][:].indirect(l_a[:, lcols]), ACT.Copy, scale=-1.0)
            for t in range(D_ON_VECTOR[blk // 2], R):
                nc.scalar.activation(gd[:, t, :], y[t][:].indirect(l_d[:, lcols]), ACT.Copy)
            tt = tts[blk]
            if blk == 0:
                sigmoid(0)
            qc = sb([P, R, P], F32, "qc%d" % blk)
            qu = sb([P, R, P], F32, "qu%d" % blk)
            for t in range(R):
                nc.scalar.activation(ncc[:, t, :], y[t][:].indirect(l_c[:, lcols]), ACT.Copy, scale=-1.0)
            nc.scalar.activation(qc[:], tt[:], ACT.Square, bias=-2.0, scale=3.0)
            nc.scalar.activation(qu[:], tt[:], ACT.Square, bias=-1.0, scale=2.0)
            turn(bg, gd, True, False)
            turn(bd, gb, True, False)
            turn(be, gb, True, False)
            turn(bg, na, False, True)
            turn(bd, ncc, False, True)
            turn(be, na, False, True)
            sums[blk] = be, bg, bd
            quads[blk] = qu, qc

        def curve(blk):
            be, bg, bd = sums[blk]
            qu, qc = quads[blk]
            tt = tts[blk]
            mm = sb([P, R, P], F32, "mm%d" % blk)
            yy = sb([P, R, P], F32, "yy%d" % blk)
            nc.vector.scalar_tensor_tensor(mm[:], bg[:], 0.125, tt[:], ALU.mult, ALU.mult)
            nc.vector.scalar_tensor_tensor(yy[:], qc[:], -7.0, bd[:], ALU.add, ALU.mult)
            nc.vector.scalar_tensor_tensor(mm[:], be[:], -0.125, mm[:], ALU.mult, ALU.add)
            nc.vector.scalar_tensor_tensor(yy[:], yy[:], 1.0 / 6.0, tt[:], ALU.mult, ALU.mult)
            nc.vector.scalar_tensor_tensor(mm[:], qu[:], -1.0, mm[:], ALU.add, ALU.mult)
            terms[blk] = mm, yy

        def backward(blk):
            cols = slice(blk * QUART, (blk + 1) * QUART)
            mm, yy = terms[blk]
            bz = bank(BACK_BANKS[blk], [P, R, QUART])
            turn(bz, yy, True, False)
            turn(bz, mm, False, True)
            nc.vector.tensor_tensor(
                zb[:, cols, :].rearrange("p (c i) t -> p c t i", i=4),
                bz[:].rearrange("p t (c i) -> p c t i", i=4),
                knots_b[blk].rearrange("p t (c i) -> p c t i", i=4), ALU.add)
            nc.vector.quantize_mx(out=zw[:, cols].bitcast(FP8X4), scales=zs[:, cols],
                                  in_=zb[:, cols, :].rearrange("p j t -> p (j t)"))

        def finish(blk):
            cols = slice(blk * QUART, (blk + 1) * QUART)
            acc = scores[blk]
            of = sb([P, R, QUART], F32, "of%d" % blk)
            nc.scalar.activation(ob[:, cols, :], acc[:].rearrange("p t j -> p j t"), ACT.Copy, scale=0.0625)
            nc.scalar.activation(of[:], acc[:], ACT.Copy, scale=0.0625)
            nc.sync.dma_start(out_rows[:, :, cols], of[:])

        def hand_on(first, last):
            cols = slice(first * QUART, (last + 1) * QUART)
            nc.vector.quantize_mx(out=ow[:, cols].bitcast(FP8X4), scales=os_[:, cols],
                                  in_=ob[:, cols, :].rearrange("p j t -> p (j t)"))
            nc.sync.dma_start(out_words[:, cols], ow[:, cols].bitcast(I32))

        pick_cand()
        fetch_pair(0)
        forward(0)
        sigmoid(1)
        sigmoid(2)
        sigmoid(3)
        fetch_pair(2)
        forward(1)
        curve(0)
        backward(0)
        forward(2)
        curve(1)
        score(0)
        backward(1)
        forward(3)
        curve(2)
        score(1)
        backward(2)
        curve(3)
        backward(3)
        score(2)
        score(3)
        finish(0)
        finish(1)
        finish(2)
        hand_on(0, 2)
        finish(3)
        hand_on(3, 3)
        for q in range(4):
            eng = nc.sync if q % 2 == 0 else nc.scalar
            eng.dma_start(out_2[0, 4 * q : 4 * q + 4, :].bitcast(I32), os_[32 * q : 32 * q + 4, :].bitcast(I32))
